import numpy as np
import ml_dtypes


def mxq(x, axis, fmt="e4m3"):
    dtype, down = {"e4m3": (ml_dtypes.float8_e4m3fn, 7), "e5m2": (ml_dtypes.float8_e5m2, 14)}[fmt]
    v = np.moveaxis(np.asarray(x, np.float32).astype(ml_dtypes.bfloat16).astype(np.float64), axis, -1)
    blocks = v.reshape(v.shape[:-1] + (-1, 32))
    amax = np.abs(blocks).max(-1, keepdims=True)
    byte = np.maximum(np.where(amax > 0, np.frexp(amax)[1] - 1 + 127, 0) - down, 1)
    scale = np.exp2(byte - 127.0)
    codes = (blocks / scale).astype(np.float32).astype(dtype).astype(np.float64)
    return np.moveaxis((codes * scale).reshape(v.shape), -1, axis)


WIDE = False


def mx_kscale(k):
    if not WIDE:
        return np.ones(k)
    levels = np.array([10, -10, 5, -5, 0])
    if k % 512:
        return np.exp2(np.random.permutation(np.resize(levels, k // 32))).repeat(32)
    a = np.empty((k // 512, 16))
    for p in range(k // 512):
        a[p, :8] = np.random.permutation(np.resize(levels, 8))
        for g in range(8):
            far = levels[np.abs(levels - a[p, g]) >= 10]
            a[p, g + 8] = far[np.random.randint(len(far))]
    return np.exp2(a.ravel()).repeat(32)


def f64(x):
    return np.asarray(x).astype(np.float64)


def striped(idx):
    return np.tile(np.asarray(idx).reshape(-1, 16).T, (8, 1)).astype(np.uint16)


def unstriped(offs):
    return offs[:16].T.reshape(-1).astype(np.int64)


E2M1 = np.array([0.0, 0.5, 1.0, 1.5, 2.0, 3.0, 4.0, 6.0, -0.0, -0.5, -1.0, -1.5, -2.0, -3.0, -4.0, -6.0])


def pack_weight(w, fmt):
    k, n = w.shape
    w = f64(np.asarray(w, np.float32).astype(ml_dtypes.bfloat16)).reshape(k // 32, 32, n)
    amax = np.abs(w).max(1)
    if fmt == "e4m3":
        byte = np.frexp(amax)[1] - 1 + 127 - 7
    else:
        mant, ex = np.frexp(amax / 6.0)
        byte = np.where(mant > 0.5, ex, ex - 1) + 127
    byte = np.clip(np.where(amax > 0, byte, 1), 1, 254)
    scaled = (w * np.exp2(127.0 - byte)[:, None, :]).reshape(k, n).astype(np.float32)
    by_word = np.ascontiguousarray(scaled.reshape(k // 512, 128, 4, n).transpose(0, 1, 3, 2))
    if fmt == "e4m3":
        words = by_word.astype(ml_dtypes.float8_e4m3fn).view(np.uint8)
    else:
        c = by_word.astype(ml_dtypes.float4_e2m1fn).view(np.uint8) & 0xF
        words = (c[..., 0::2] | (c[..., 1::2] << 4)).reshape(k // 512, 128, 2 * n)
    return np.ascontiguousarray(words), np.ascontiguousarray(byte.astype(np.uint8).reshape(k // 512, 16, n))


def unpack_weight(words, scales, fmt):
    g, _, n = scales.shape
    words = np.ascontiguousarray(words).reshape(g, 128, n, -1)
    if fmt == "e4m3":
        vals = words.view(ml_dtypes.float8_e4m3fn).astype(np.float64)
    else:
        nib = np.empty((g, 128, n, 4), np.uint8)
        nib[..., 0::2] = words & 0xF
        nib[..., 1::2] = words >> 4
        vals = E2M1[nib]
    vals = vals * np.repeat(np.exp2(scales.astype(np.float64) - 127.0), 8, axis=1)[..., None]
    return vals.transpose(0, 1, 3, 2).reshape(g * 512, n)


D, T, I, Q, E = 512, 2048, 512, 128, 512


def setup_inputs():
    n = np.random.standard_normal
    idx = np.random.permutation(T)[:I]
    fd = mx_kscale(D)
    fi = mx_kscale(I)
    ti = np.ones(T)
    ti[idx] = fi
    keysp = pack_weight(n((D, T)) / fd[:, None], "e4m3")
    return {
        "query": (n((D, Q)) * 0.25 / np.sqrt(D) * fd[:, None]).astype(np.float32),
        "avoid": (n((D, Q)) * 1.0 / np.sqrt(D) * fd[:, None]).astype(np.float32),
        "keys_words": keysp[0],
        "keys_scales": keysp[1],
        "aver": (np.random.uniform(0.5, 1.5, (Q, 1))).astype(np.float32),
        "size": (np.random.uniform(0.5, 2.0, (1, I)) * fi).astype(np.float32),
        "vals": (n((E, T)) / ti).astype(np.float32),
        "offs": striped(idx),
    }


def reference(query, avoid, keys_words, keys_scales, aver, size, vals, offs):
    idx = unstriped(offs)
    keysu = unpack_weight(keys_words, keys_scales, "e4m3")
    queryq = mxq(f64(query), 0, "e4m3")
    keysidxg = keysu[:, idx]
    a = queryq.T @ keysidxg
    avoidq = mxq(f64(avoid), 0, "e4m3")
    b = avoidq.T @ keysidxg
    s = a - np.maximum(b, 0.0) * f64(aver)
    p = np.exp(s - np.max(s, axis=1, keepdims=True))
    w = p * f64(size) / np.sum(p, axis=1, keepdims=True)
    wt = w.T
    vt = f64(vals)[:, idx].T
    wtq = mxq(wt, 0, "e4m3")
    vtq = mxq(vt, 0, "e4m3")
    o = wtq.T @ vtq
    return o

@@ -1,0 +1,137 @@
+from contextlib import ExitStack
+
+import concourse.mybir as mybir
+from concourse.masks import make_identity
+
+D, T, I, Q, E = 512, 2048, 512, 128, 512
+FLOPS = 2 * Q * I * (2 * D + E)
+
+F32 = mybir.dt.float32
+BF16 = mybir.dt.bfloat16
+I32 = mybir.dt.int32
+U32 = mybir.dt.uint32
+U16 = mybir.dt.uint16
+U8 = mybir.dt.uint8
+FP8X4 = mybir.dt.float8_e4m3fn_x4
+ALU = mybir.AluOpType
+ACT = mybir.ActivationFunctionType
+
+P = 128
+PACK = 4
+
+
+def tile_attend_antiquery_kernel(tc, query, avoid, keys_words, keys_scales, aver, size, vals, offs, out):
+    nc = tc.nc
+    with ExitStack() as ctx:
+        sb = ctx.enter_context(tc.tile_pool(name="sb", bufs=1))
+        ps = ctx.enter_context(tc.psum_pool(name="ps", bufs=1))
+
+        offsets = sb.tile([P, I // 16], U16, name="offsets")
+        key_words = sb.tile([P, T], U32, name="key_words", tag="slot3", align_bytes=64)
+        key_bytes = sb.tile([P, T], U8, name="key_bytes", align_bytes=64)
+        rows = sb.tile([P, P], F32, name="rows", align_bytes=64)
+        ident = sb.tile([P, P], F32, name="ident", align_bytes=64)
+        raw = [sb.tile([P, PACK, Q], F32, name="raw%d" % n, tag="slot%d" % (n + 1), align_bytes=64) for n in range(2)]
+        aver_col = sb.tile([P, 1], F32, name="aver_col")
+        warm = sb.tile([P, 1], F32, name="warm")
+
+        nc.gpsimd.memset(key_bytes[:].bitcast(I32), 0)
+        nc.gpsimd.memset(rows[:], 0.0)
+        nc.scalar.dma_start(aver_col[:], aver)
+        make_identity(nc, ident[:])
+
+        def load_vals(j):
+            window = sb.tile([P, T], F32, name="pool%d" % j, tag="slot%d" % j, align_bytes=64)
+            nc.sync.dma_start(window[:], vals[j * P : (j + 1) * P, :])
+            return window
+
+        nc.sync.dma_start(offsets[:], offs)
+        nc.sync.dma_start(key_words[:].bitcast(I32), keys_words[0].rearrange("p n t -> p (n t)").bitcast(I32))
+        for quad in range(4):
+            nc.scalar.dma_start(
+                key_bytes[32 * quad : 32 * quad + 4, :].bitcast(I32),
+                keys_scales[0, 4 * quad : 4 * quad + 4, :].bitcast(I32),
+            )
+        for n, src in enumerate((avoid, query)):
+            nc.sync.dma_start(raw[n][:], src.rearrange("(p j) q -> p j q", j=PACK))
+        pool = [load_vals(0)]
+        nc.scalar.activation(warm[:], rows[:, 0:1], ACT.Exp)
+        nc.scalar.dma_start(rows[0:4, :], size.rearrange("o (c n) -> (o c) n", n=P))
+
+        k_words = sb.tile([P, I], U32, name="k_words", align_bytes=64)
+        k_bytes = sb.tile([P, I], U8, name="k_bytes", align_bytes=64)
+        nc.vector.tensor_copy(k_bytes[:], key_bytes[:].indirect(offsets[:]))
+        nc.vector.tensor_copy(k_words[:], key_words[:].indirect(offsets[:]))
+
+        def quantise(name, grouped):
+            codes = sb.tile([P, P], U32, name=name + "_codes", align_bytes=64)
+            scales = sb.tile([P, P], U8, name=name + "_scales", align_bytes=64)
+            nc.vector.quantize_mx(out=codes[:].bitcast(FP8X4), scales=scales[:], in_=grouped[:])
+            return codes, scales
+
+        scores = []
+        for n in range(2):
+            grouped = sb.tile([P, Q * PACK], BF16, name="qg%d" % n, align_bytes=64)
+            nc.scalar.copy(grouped[:].rearrange("p (q j) -> p q j", j=PACK), raw[n][:].rearrange("p j q -> p q j"))
+            codes, scales = quantise("q%d" % n, grouped)
+            bank = ps.tile([P, I], F32, name="score%d" % n)
+            nc.tensor.matmul_mx(
+                out=bank[:], lhsT=codes[:].bitcast(FP8X4), lhsT_scale=scales[:],
+                rhs=k_words[:].bitcast(FP8X4), rhs_scale=k_bytes[:], start=True, stop=True,
+            )
+            scores.append(bank)
+        b_ps, a_ps = scores
+        pool.extend(load_vals(j) for j in range(1, E // P))
+
+        cols_ps = ps.tile([P, I], F32, name="small")
+        nc.tensor.transpose(cols_ps[:, 0:P], rows[:], ident[:])
+        cols = sb.tile([P, 4], F32, name="cols", align_bytes=64)
+        nc.scalar.copy(cols[:], cols_ps[:, 0:4])
+        size_ps = ps.tile([P, I], F32, name="small")
+        for c in range(I // P):
+            nc.tensor.transpose(size_ps[:, c * P : (c + 1) * P], cols[:, c : c + 1].to_broadcast([P, P]), ident[:])
+
+        relu_b = sb.tile([P, I], F32, name="relu_b", tag="work0", align_bytes=64)
+        nc.scalar.activation(relu_b[:], b_ps[:], ACT.Relu)
+        neg_s = sb.tile([P, I], F32, name="neg_s", align_bytes=64)
+        nc.vector.scalar_tensor_tensor(neg_s[:], relu_b[:], aver_col[:], a_ps[:], ALU.mult, ALU.subtract)
+        neg_max = sb.tile([P, 1], F32, name="neg_max")
+        nc.vector.tensor_reduce(neg_max[:], neg_s[:], mybir.AxisListType.X, ALU.min)
+        p = sb.tile([P, I], F32, name="p", tag="work1", align_bytes=64)
+        total = sb.tile([P, 1], F32, name="total")
+        nc.scalar.activation(p[:], neg_s[:], ACT.Exp, bias=neg_max[:], scale=-1.0, accum_out=total[:])
+
+        def turn(name, src, tag):
+            words = src[:].bitcast(F32)
+            bank = ps.tile([P, 2, P], F32, name="turn", bufs=2)
+            for u in range(2):
+                nc.tensor.transpose(bank[:, u, :], words[:, u::2], ident[:])
+            grouped = sb.tile([P, P * PACK], BF16, name=name + "_grouped", tag=tag, align_bytes=64)
+            nc.scalar.copy(grouped[:].bitcast(F32).rearrange("p (x u) -> p x u", u=2), bank[:].rearrange("p u x -> p x u"))
+            return grouped
+
+        def gather(j):
+            picked = sb.tile([P, I], BF16, name="picked%d" % j, tag="work%d" % j, align_bytes=64)
+            nc.vector.tensor_copy(picked[:], pool[j][:].indirect(offsets[:]))
+            return turn("v%d" % j, picked, "vg%d" % j)
+
+        v_grouped = gather(0)
+
+        inv = sb.tile([P, 1], F32, name="inv")
+        nc.vector.reciprocal(inv[:], total[:])
+        w = sb.tile([P, I], BF16, name="w", align_bytes=64)
+        nc.vector.scalar_tensor_tensor(w[:], p[:], inv[:], size_ps[:], ALU.mult, ALU.mult)
+        w_codes, w_scales = quantise("w", turn("w", w, "work2"))
+
+        for j in range(E // P):
+            v_codes, v_scales = quantise("v%d" % j, v_grouped)
+            if j + 1 < E // P:
+                v_grouped = gather(j + 1)
+            acc = ps.tile([P, P], F32, name="acc", bufs=2)
+            nc.tensor.matmul_mx(
+                out=acc[:], lhsT=w_codes[:].bitcast(FP8X4), lhsT_scale=w_scales[:],
+                rhs=v_codes[:].bitcast(FP8X4), rhs_scale=v_scales[:], start=True, stop=True,
+            )
+            result = sb.tile([P, P], F32, name="result%d" % j, align_bytes=64)
+            nc.scalar.copy(result[:], acc[:])
+            nc.sync.dma_start(out[:, j * P : (j + 1) * P], result[:])

@@ -1,7 +1,6 @@
 from contextlib import ExitStack
 
 import concourse.mybir as mybir
-from concourse.masks import make_identity
 
 D, T, I, Q, E = 512, 2048, 512, 128, 512
 FLOPS = 2 * Q * I * (2 * D + E)
@@ -18,6 +17,7 @@ ACT = mybir.ActivationFunctionType
 
 P = 128
 PACK = 4
+WINDOW_BYTES = 4 * T
 
 
 def tile_attend_antiquery_kernel(tc, query, avoid, keys_words, keys_scales, aver, size, vals, offs, out):
@@ -27,26 +27,29 @@ def tile_attend_antiquery_kernel(tc, query, avoid, keys_words, keys_scales, aver
         ps = ctx.enter_context(tc.psum_pool(name="ps", bufs=1))
 
         offsets = sb.tile([P, I // 16], U16, name="offsets")
-        key_words = sb.tile([P, T], U32, name="key_words", tag="slot3", align_bytes=64)
-        key_bytes = sb.tile([P, T], U8, name="key_bytes", align_bytes=64)
-        rows = sb.tile([P, P], F32, name="rows", align_bytes=64)
+        key_bytes = sb.tile([P, T], U8, name="key_bytes", tag="key_slot", align_bytes=64)
         ident = sb.tile([P, P], F32, name="ident", align_bytes=64)
-        raw = [sb.tile([P, PACK, Q], F32, name="raw%d" % n, tag="slot%d" % (n + 1), align_bytes=64) for n in range(2)]
-        aver_col = sb.tile([P, 1], F32, name="aver_col")
+        raw = [sb.tile([P, PACK, Q], F32, name="raw%d" % n, align_bytes=64) for n in range(2)]
         warm = sb.tile([P, 1], F32, name="warm")
 
         nc.gpsimd.memset(key_bytes[:].bitcast(I32), 0)
-        nc.gpsimd.memset(rows[:], 0.0)
-        nc.scalar.dma_start(aver_col[:], aver)
-        make_identity(nc, ident[:])
+        with tc.tile_pool(name="setup", bufs=1) as setup:
+            zeros = setup.tile([P, P], F32, name="zeros")
+            nc.vector.memset(zeros[:], 0.0)
+            nc.gpsimd.affine_select(
+                out=ident[:], in_=zeros[:], compare_op=ALU.not_equal, fill=1.0, base=0, pattern=[[-1, P]], channel_multiplier=1
+            )
+        windows = ctx.enter_context(tc.tile_pool(name="windows", bufs=1))
+        key_words = windows.tile([P, T], U32, name="key_words", offset=4 * WINDOW_BYTES, align_bytes=64)
+        aver_col = windows.tile([P, 1], F32, name="aver_col", offset=5 * WINDOW_BYTES, align_bytes=64)
+        cols = windows.tile([P, PACK], F32, name="cols", offset=5 * WINDOW_BYTES + 64, align_bytes=64)
 
         def load_vals(j):
-            window = sb.tile([P, T], F32, name="pool%d" % j, tag="slot%d" % j, align_bytes=64)
+            window = windows.tile([P, T], F32, name="pool%d" % j, offset=j * WINDOW_BYTES, align_bytes=64)
             nc.sync.dma_start(window[:], vals[j * P : (j + 1) * P, :])
             return window
 
         nc.sync.dma_start(offsets[:], offs)
-        nc.sync.dma_start(key_words[:].bitcast(I32), keys_words[0].rearrange("p n t -> p (n t)").bitcast(I32))
         for quad in range(4):
             nc.scalar.dma_start(
                 key_bytes[32 * quad : 32 * quad + 4, :].bitcast(I32),
@@ -54,20 +57,29 @@ def tile_attend_antiquery_kernel(tc, query, avoid, keys_words, keys_scales, aver
             )
         for n, src in enumerate((avoid, query)):
             nc.sync.dma_start(raw[n][:], src.rearrange("(p j) q -> p j q", j=PACK))
-        pool = [load_vals(0)]
-        nc.scalar.activation(warm[:], rows[:, 0:1], ACT.Exp)
-        nc.scalar.dma_start(rows[0:4, :], size.rearrange("o (c n) -> (o c) n", n=P))
+        nc.sync.dma_start(key_words[:].bitcast(I32), keys_words[0].rearrange("p n t -> p (n t)").bitcast(I32))
+        nc.sync.dma_start(aver_col[:], aver)
+        nc.sync.dma_start(cols[:], size.rearrange("o (p c) -> (o p) c", c=PACK))
+        pool = [load_vals(j) for j in range(E // P)]
+        nc.scalar.activation(warm[:], ident[:, 0:1], ACT.Exp)
 
-        k_words = sb.tile([P, I], U32, name="k_words", align_bytes=64)
+        k_words = sb.tile([P, I], U32, name="k_words", tag="key_slot", align_bytes=64)
         k_bytes = sb.tile([P, I], U8, name="k_bytes", align_bytes=64)
         nc.vector.tensor_copy(k_bytes[:], key_bytes[:].indirect(offsets[:]))
         nc.vector.tensor_copy(k_words[:], key_words[:].indirect(offsets[:]))
 
-        def quantise(name, grouped):
-            codes = sb.tile([P, P], U32, name=name + "_codes", align_bytes=64)
+        def quantise(name, grouped, place=None):
+            if place is None:
+                codes = sb.tile([P, P], U32, name=name + "_codes", align_bytes=64)
+            else:
+                codes = windows.tile([P, P], U32, name=name + "_codes", offset=3 * WINDOW_BYTES + place * 4 * P, align_bytes=64)
             scales = sb.tile([P, P], U8, name=name + "_scales", align_bytes=64)
             nc.vector.quantize_mx(out=codes[:].bitcast(FP8X4), scales=scales[:], in_=grouped[:])
             return codes, scales
+
+        size_ps = ps.tile([P, I], F32, name="small")
+        for c in range(I // P):
+            nc.tensor.transpose(size_ps[:, c * P : (c + 1) * P], cols[:, c : c + 1].to_broadcast([P, P]), ident[:])
 
         scores = []
         for n in range(2):
@@ -81,52 +93,22 @@ def tile_attend_antiquery_kernel(tc, query, avoid, keys_words, keys_scales, aver
             )
             scores.append(bank)
         b_ps, a_ps = scores
-        pool.extend(load_vals(j) for j in range(1, E // P))
 
-        cols_ps = ps.tile([P, I], F32, name="small")
-        nc.tensor.transpose(cols_ps[:, 0:P], rows[:], ident[:])
-        cols = sb.tile([P, 4], F32, name="cols", align_bytes=64)
-        nc.scalar.copy(cols[:], cols_ps[:, 0:4])
-        size_ps = ps.tile([P, I], F32, name="small")
-        for c in range(I // P):
-            nc.tensor.transpose(size_ps[:, c * P : (c + 1) * P], cols[:, c : c + 1].to_broadcast([P, P]), ident[:])
-
-        relu_b = sb.tile([P, I], F32, name="relu_b", tag="work0", align_bytes=64)
-        nc.scalar.activation(relu_b[:], b_ps[:], ACT.Relu)
-        neg_s = sb.tile([P, I], F32, name="neg_s", align_bytes=64)
-        nc.vector.scalar_tensor_tensor(neg_s[:], relu_b[:], aver_col[:], a_ps[:], ALU.mult, ALU.subtract)
-        neg_max = sb.tile([P, 1], F32, name="neg_max")
-        nc.vector.tensor_reduce(neg_max[:], neg_s[:], mybir.AxisListType.X, ALU.min)
-        p = sb.tile([P, I], F32, name="p", tag="work1", align_bytes=64)
-        total = sb.tile([P, 1], F32, name="total")
-        nc.scalar.activation(p[:], neg_s[:], ACT.Exp, bias=neg_max[:], scale=-1.0, accum_out=total[:])
-
-        def turn(name, src, tag):
+        def turn(name, src):
             words = src[:].bitcast(F32)
             bank = ps.tile([P, 2, P], F32, name="turn", bufs=2)
             for u in range(2):
                 nc.tensor.transpose(bank[:, u, :], words[:, u::2], ident[:])
-            grouped = sb.tile([P, P * PACK], BF16, name=name + "_grouped", tag=tag, align_bytes=64)
+            grouped = sb.tile([P, P * PACK], BF16, name=name + "_grouped", align_bytes=64)
             nc.scalar.copy(grouped[:].bitcast(F32).rearrange("p (x u) -> p x u", u=2), bank[:].rearrange("p u x -> p x u"))
             return grouped
 
         def gather(j):
-            picked = sb.tile([P, I], BF16, name="picked%d" % j, tag="work%d" % j, align_bytes=64)
+            picked = sb.tile([P, I], BF16, name="picked%d" % j, align_bytes=64)
             nc.vector.tensor_copy(picked[:], pool[j][:].indirect(offsets[:]))
-            return turn("v%d" % j, picked, "vg%d" % j)
+            return picked
 
-        v_grouped = gather(0)
-
-        inv = sb.tile([P, 1], F32, name="inv")
-        nc.vector.reciprocal(inv[:], total[:])
-        w = sb.tile([P, I], BF16, name="w", align_bytes=64)
-        nc.vector.scalar_tensor_tensor(w[:], p[:], inv[:], size_ps[:], ALU.mult, ALU.mult)
-        w_codes, w_scales = quantise("w", turn("w", w, "work2"))
-
-        for j in range(E // P):
-            v_codes, v_scales = quantise("v%d" % j, v_grouped)
-            if j + 1 < E // P:
-                v_grouped = gather(j + 1)
+        def product(j, v_codes, v_scales):
             acc = ps.tile([P, P], F32, name="acc", bufs=2)
             nc.tensor.matmul_mx(
                 out=acc[:], lhsT=w_codes[:].bitcast(FP8X4), lhsT_scale=w_scales[:],
@@ -135,3 +117,34 @@ def tile_attend_antiquery_kernel(tc, query, avoid, keys_words, keys_scales, aver
             result = sb.tile([P, P], F32, name="result%d" % j, align_bytes=64)
             nc.scalar.copy(result[:], acc[:])
             nc.sync.dma_start(out[:, j * P : (j + 1) * P], result[:])
+
+        relu_b = sb.tile([P, I], F32, name="relu_b", align_bytes=64)
+        nc.scalar.activation(relu_b[:], b_ps[:], ACT.Relu)
+        picked0 = gather(0)
+        neg_s = windows.tile([P, I], F32, name="neg_s", offset=0, align_bytes=64)
+        nc.vector.scalar_tensor_tensor(neg_s[:], relu_b[:], aver_col[:], a_ps[:], ALU.mult, ALU.subtract)
+        neg_max = sb.tile([P, 1], F32, name="neg_max")
+        nc.vector.tensor_reduce(neg_max[:], neg_s[:], mybir.AxisListType.X, ALU.min)
+        grouped0 = turn("v0", picked0)
+        p = sb.tile([P, I], F32, name="p", align_bytes=64)
+        total = sb.tile([P, 1], F32, name="total")
+        nc.scalar.activation(p[:], neg_s[:], ACT.Exp, bias=neg_max[:], scale=-1.0, accum_out=total[:])
+        grouped1 = turn("v1", gather(1))
+        inv = windows.tile([P, 1], F32, name="inv", offset=WINDOW_BYTES, align_bytes=64)
+        nc.vector.reciprocal(inv[:], total[:])
+        v0 = quantise("v0", grouped0)
+        w = sb.tile([P, I], BF16, name="w", align_bytes=64)
+        nc.vector.scalar_tensor_tensor(
+            w[:].rearrange("q (n c) -> q n c", c=PACK), p[:].rearrange("q (n c) -> q n c", c=PACK), inv[:],
+            size_ps[:].rearrange("q (c n) -> q n c", c=PACK), ALU.mult, ALU.mult,
+        )
+        w_grouped = turn("w", w)
+        grouped2 = turn("v2", gather(2))
+        grouped3 = turn("v3", gather(3))
+        w_codes, w_scales = quantise("w", w_grouped, 0)
+        v1 = quantise("v1", grouped1, 1)
+        product(0, *v0)
+        v2 = quantise("v2", grouped2, 2)
+        product(1, *v1)
+        product(2, *v2)
+        product(3, *quantise("v3", grouped3))

@@ -1,6 +1,7 @@
 from contextlib import ExitStack
 
 import concourse.mybir as mybir
+from concourse.masks import make_identity
 
 D, T, I, Q, E = 512, 2048, 512, 128, 512
 FLOPS = 2 * Q * I * (2 * D + E)
@@ -17,7 +18,9 @@ ACT = mybir.ActivationFunctionType
 
 P = 128
 PACK = 4
+QUADRANT = 32
 WINDOW_BYTES = 4 * T
+ALIGN = 64
 
 
 def tile_attend_antiquery_kernel(tc, query, avoid, keys_words, keys_scales, aver, size, vals, offs, out):
@@ -27,124 +30,125 @@ def tile_attend_antiquery_kernel(tc, query, avoid, keys_words, keys_scales, aver
         ps = ctx.enter_context(tc.psum_pool(name="ps", bufs=1))
 
         offsets = sb.tile([P, I // 16], U16, name="offsets")
-        key_bytes = sb.tile([P, T], U8, name="key_bytes", tag="key_slot", align_bytes=64)
-        ident = sb.tile([P, P], F32, name="ident", align_bytes=64)
-        raw = [sb.tile([P, PACK, Q], F32, name="raw%d" % n, align_bytes=64) for n in range(2)]
-        warm = sb.tile([P, 1], F32, name="warm")
+        key_words = sb.tile([P, T], U32, name="key_words", tag="keys", align_bytes=ALIGN)
+        key_bytes = sb.tile([P, T], U8, name="key_bytes", align_bytes=ALIGN)
+        rows = [sb.tile([P, PACK, Q], F32, name="rows%d" % n) for n in range(2)]
+        neg_aver = sb.tile([P, 1], F32, name="neg_aver")
+        ident = sb.tile([P, P], F32, name="ident")
 
-        nc.gpsimd.memset(key_bytes[:].bitcast(I32), 0)
-        with tc.tile_pool(name="setup", bufs=1) as setup:
-            zeros = setup.tile([P, P], F32, name="zeros")
-            nc.vector.memset(zeros[:], 0.0)
-            nc.gpsimd.affine_select(
-                out=ident[:], in_=zeros[:], compare_op=ALU.not_equal, fill=1.0, base=0, pattern=[[-1, P]], channel_multiplier=1
-            )
-        windows = ctx.enter_context(tc.tile_pool(name="windows", bufs=1))
-        key_words = windows.tile([P, T], U32, name="key_words", offset=4 * WINDOW_BYTES, align_bytes=64)
-        aver_col = windows.tile([P, 1], F32, name="aver_col", offset=5 * WINDOW_BYTES, align_bytes=64)
-        cols = windows.tile([P, PACK], F32, name="cols", offset=5 * WINDOW_BYTES + 64, align_bytes=64)
+        nc.vector.memset(key_bytes[:].bitcast(I32), 0)
+        make_identity(nc, ident[:])
+        with tc.tile_pool(name="early", bufs=1) as early:
+            aver_col = early.tile([P, 1], F32, name="aver_col")
+            nc.scalar.dma_start(aver_col[:], aver)
+            nc.sync.dma_start(offsets[:], offs)
+            nc.sync.dma_start(key_words[:].bitcast(I32), keys_words[0].rearrange("p t r -> p (t r)").bitcast(I32))
+            for n, source in enumerate((avoid, query)):
+                nc.sync.dma_start(rows[n][:], source.rearrange("(p r) q -> p r q", r=PACK))
+            for quad in range(P // QUADRANT):
+                nc.scalar.dma_start(
+                    key_bytes[QUADRANT * quad : QUADRANT * quad + 4, :].bitcast(I32),
+                    keys_scales[0, 4 * quad : 4 * quad + 4, :].bitcast(I32),
+                )
+            nc.vector.tensor_scalar_mul(neg_aver[:], aver_col[:], -1.0)
 
-        def load_vals(j):
-            window = windows.tile([P, T], F32, name="pool%d" % j, offset=j * WINDOW_BYTES, align_bytes=64)
-            nc.sync.dma_start(window[:], vals[j * P : (j + 1) * P, :])
-            return window
+        late = ctx.enter_context(tc.tile_pool(name="late", bufs=1))
 
-        nc.sync.dma_start(offsets[:], offs)
-        for quad in range(4):
-            nc.scalar.dma_start(
-                key_bytes[32 * quad : 32 * quad + 4, :].bitcast(I32),
-                keys_scales[0, 4 * quad : 4 * quad + 4, :].bitcast(I32),
-            )
-        for n, src in enumerate((avoid, query)):
-            nc.sync.dma_start(raw[n][:], src.rearrange("(p j) q -> p j q", j=PACK))
-        nc.sync.dma_start(key_words[:].bitcast(I32), keys_words[0].rearrange("p n t -> p (n t)").bitcast(I32))
-        nc.sync.dma_start(aver_col[:], aver)
-        nc.sync.dma_start(cols[:], size.rearrange("o (p c) -> (o p) c", c=PACK))
-        pool = [load_vals(j) for j in range(E // P)]
-        nc.scalar.activation(warm[:], ident[:, 0:1], ACT.Exp)
+        def late_tile(name, shape, dtype, window):
+            return late.tile(shape, dtype, name=name, offset=window * WINDOW_BYTES, align_bytes=ALIGN)
 
-        k_words = sb.tile([P, I], U32, name="k_words", tag="key_slot", align_bytes=64)
-        k_bytes = sb.tile([P, I], U8, name="k_bytes", align_bytes=64)
-        nc.vector.tensor_copy(k_bytes[:], key_bytes[:].indirect(offsets[:]))
-        nc.vector.tensor_copy(k_words[:], key_words[:].indirect(offsets[:]))
+        windows = [late_tile("window%d" % j, [P, T], F32, j) for j in range(E // P)]
+        size_cols = late_tile("size_cols", [P, PACK], F32, E // P)
+        for j in range(E // P):
+            nc.sync.dma_start(windows[j][:], vals[j * P : (j + 1) * P, :])
+            if j == 0:
+                nc.sync.dma_start(size_cols[:], size.rearrange("o (p r) -> (o p) r", r=PACK))
 
-        def quantise(name, grouped, place=None):
-            if place is None:
-                codes = sb.tile([P, P], U32, name=name + "_codes", align_bytes=64)
-            else:
-                codes = windows.tile([P, P], U32, name=name + "_codes", offset=3 * WINDOW_BYTES + place * 4 * P, align_bytes=64)
-            scales = sb.tile([P, P], U8, name=name + "_scales", align_bytes=64)
+        def quantise(name, grouped, codes):
+            scales = sb.tile(list(codes.shape), U8, name=name + "_scales", align_bytes=ALIGN)
             nc.vector.quantize_mx(out=codes[:].bitcast(FP8X4), scales=scales[:], in_=grouped[:])
             return codes, scales
 
-        size_ps = ps.tile([P, I], F32, name="small")
-        for c in range(I // P):
-            nc.tensor.transpose(size_ps[:, c * P : (c + 1) * P], cols[:, c : c + 1].to_broadcast([P, P]), ident[:])
-
-        scores = []
-        for n in range(2):
-            grouped = sb.tile([P, Q * PACK], BF16, name="qg%d" % n, align_bytes=64)
-            nc.scalar.copy(grouped[:].rearrange("p (q j) -> p q j", j=PACK), raw[n][:].rearrange("p j q -> p q j"))
-            codes, scales = quantise("q%d" % n, grouped)
-            bank = ps.tile([P, I], F32, name="score%d" % n)
+        def product(bank, stationary, moving):
             nc.tensor.matmul_mx(
-                out=bank[:], lhsT=codes[:].bitcast(FP8X4), lhsT_scale=scales[:],
-                rhs=k_words[:].bitcast(FP8X4), rhs_scale=k_bytes[:], start=True, stop=True,
+                out=bank, lhsT=stationary[0].bitcast(FP8X4), lhsT_scale=stationary[1],
+                rhs=moving[0].bitcast(FP8X4), rhs_scale=moving[1], start=True, stop=True,
             )
-            scores.append(bank)
-        b_ps, a_ps = scores
 
-        def turn(name, src):
-            words = src[:].bitcast(F32)
+        k_words = sb.tile([P, I], U32, name="k_words", align_bytes=ALIGN)
+        nc.vector.tensor_copy(k_words[:], key_words[:].indirect(offsets[:]))
+        k_bytes = sb.tile([P, I], U8, name="k_bytes", tag="keys", align_bytes=ALIGN)
+        nc.vector.tensor_copy(k_bytes[:], key_bytes[:].indirect(offsets[:]))
+
+        rows_mx = []
+        for n in range(2):
+            grouped = sb.tile([P, Q * PACK], BF16, name="rows_grouped%d" % n, align_bytes=ALIGN)
+            nc.scalar.activation(
+                grouped[:].rearrange("p (q r) -> p q r", r=PACK), rows[n][:].rearrange("p r q -> p q r"), ACT.Copy
+            )
+            codes, scales = quantise("rows%d" % n, grouped, sb.tile([P, Q], U32, name="rows%d_codes" % n, align_bytes=ALIGN))
+            rows_mx.append((codes[:], scales[:]))
+        relu_b = sb.tile([P, I], F32, name="relu_b")
+        for half in range(2):
+            slots = slice(half * I // 2, (half + 1) * I // 2)
+            b_bank = ps.tile([P, I // 2], F32, name="b_bank", tag="shared%d" % half)
+            product(b_bank[:], rows_mx[0], (k_words[:, slots], k_bytes[:, slots]))
+            nc.scalar.activation(relu_b[:, slots], b_bank[:], ACT.Relu)
+        a_bank = ps.tile([P, I], F32, name="a_bank", tag="shared2")
+        product(a_bank[:], rows_mx[1], (k_words[:], k_bytes[:]))
+
+        size_bank = ps.tile([P, PACK, P], F32, name="size_bank")
+        for r in range(PACK):
+            nc.tensor.transpose(size_bank[:, r, :], size_cols[:, r : r + 1].to_broadcast([P, P]), ident[:])
+
+        def turn(source, grouped):
+            words = source[:].bitcast(F32)
             bank = ps.tile([P, 2, P], F32, name="turn", bufs=2)
             for u in range(2):
                 nc.tensor.transpose(bank[:, u, :], words[:, u::2], ident[:])
-            grouped = sb.tile([P, P * PACK], BF16, name=name + "_grouped", align_bytes=64)
-            nc.scalar.copy(grouped[:].bitcast(F32).rearrange("p (x u) -> p x u", u=2), bank[:].rearrange("p u x -> p x u"))
-            return grouped
+            nc.scalar.copy(grouped.bitcast(F32).rearrange("p (x u) -> p x u", u=2), bank[:].rearrange("p u x -> p x u"))
 
-        def gather(j):
-            picked = sb.tile([P, I], BF16, name="picked%d" % j, align_bytes=64)
-            nc.vector.tensor_copy(picked[:], pool[j][:].indirect(offsets[:]))
+        def gather(j, picked):
+            nc.vector.tensor_copy(picked[:], windows[j][:].indirect(offsets[:]))
             return picked
 
-        def product(j, v_codes, v_scales):
-            acc = ps.tile([P, P], F32, name="acc", bufs=2)
-            nc.tensor.matmul_mx(
-                out=acc[:], lhsT=w_codes[:].bitcast(FP8X4), lhsT_scale=w_scales[:],
-                rhs=v_codes[:].bitcast(FP8X4), rhs_scale=v_scales[:], start=True, stop=True,
-            )
-            result = sb.tile([P, P], F32, name="result%d" % j, align_bytes=64)
-            nc.scalar.copy(result[:], acc[:])
-            nc.sync.dma_start(out[:, j * P : (j + 1) * P], result[:])
+        first = sb.tile([P, 2 * I], BF16, name="first", align_bytes=ALIGN)
+        middle = sb.tile([P, 2 * I], BF16, name="middle", align_bytes=ALIGN)
+        last = sb.tile([P, I], BF16, name="last", align_bytes=ALIGN)
 
-        relu_b = sb.tile([P, I], F32, name="relu_b", align_bytes=64)
-        nc.scalar.activation(relu_b[:], b_ps[:], ACT.Relu)
-        picked0 = gather(0)
-        neg_s = windows.tile([P, I], F32, name="neg_s", offset=0, align_bytes=64)
-        nc.vector.scalar_tensor_tensor(neg_s[:], relu_b[:], aver_col[:], a_ps[:], ALU.mult, ALU.subtract)
+        picked0 = gather(0, sb.tile([P, I], BF16, name="picked0"))
+        s = late_tile("s", [P, I], F32, 0)
+        nc.vector.scalar_tensor_tensor(s[:], relu_b[:], neg_aver[:], a_bank[:], ALU.mult, ALU.add)
         neg_max = sb.tile([P, 1], F32, name="neg_max")
-        nc.vector.tensor_reduce(neg_max[:], neg_s[:], mybir.AxisListType.X, ALU.min)
-        grouped0 = turn("v0", picked0)
-        p = sb.tile([P, I], F32, name="p", align_bytes=64)
+        nc.vector.tensor_reduce(neg_max[:], s[:], mybir.AxisListType.X, ALU.max, negate=True)
+        turn(picked0, first[:, I:])
+        p = sb.tile([P, I], F32, name="p")
         total = sb.tile([P, 1], F32, name="total")
-        nc.scalar.activation(p[:], neg_s[:], ACT.Exp, bias=neg_max[:], scale=-1.0, accum_out=total[:])
-        grouped1 = turn("v1", gather(1))
-        inv = windows.tile([P, 1], F32, name="inv", offset=WINDOW_BYTES, align_bytes=64)
-        nc.vector.reciprocal(inv[:], total[:])
-        v0 = quantise("v0", grouped0)
-        w = sb.tile([P, I], BF16, name="w", align_bytes=64)
+        nc.scalar.activation(p[:], s[:], ACT.Exp, bias=neg_max[:], accum_out=total[:])
+        turn(gather(1, late_tile("picked1", [P, I], BF16, E // P)), middle[:, :I])
+        inverse = late_tile("inverse", [P, 1], F32, 1)
+        nc.vector.reciprocal(inverse[:], total[:])
+        w = sb.tile([P, I], BF16, name="w", align_bytes=ALIGN)
         nc.vector.scalar_tensor_tensor(
-            w[:].rearrange("q (n c) -> q n c", c=PACK), p[:].rearrange("q (n c) -> q n c", c=PACK), inv[:],
-            size_ps[:].rearrange("q (c n) -> q n c", c=PACK), ALU.mult, ALU.mult,
+            w[:].rearrange("q (p r) -> q p r", r=PACK), p[:].rearrange("q (p r) -> q p r", r=PACK), inverse[:],
+            size_bank[:].rearrange("q r p -> q p r"), ALU.mult, ALU.mult,
         )
-        w_grouped = turn("w", w)
-        grouped2 = turn("v2", gather(2))
-        grouped3 = turn("v3", gather(3))
-        w_codes, w_scales = quantise("w", w_grouped, 0)
-        v1 = quantise("v1", grouped1, 1)
-        product(0, *v0)
-        v2 = quantise("v2", grouped2, 2)
-        product(1, *v1)
-        product(2, *v2)
-        product(3, *quantise("v3", grouped3))
+        turn(w, first[:, :I])
+        turn(gather(2, sb.tile([P, I], BF16, name="picked2")), middle[:, I:])
+        turn(gather(3, sb.tile([P, I], BF16, name="picked3", tag="tail")), last[:])
+
+        first_codes, first_scales = quantise("first", first, late_tile("first_codes", [P, 2 * P], U32, 3))
+        middle_codes, middle_scales = quantise("middle", middle, late.tile([P, 2 * P], U32, name="middle_codes", offset=3 * WINDOW_BYTES + 8 * P, align_bytes=ALIGN))
+        last_codes, last_scales = quantise("last", last, sb.tile([P, P], U32, name="last_codes", align_bytes=ALIGN))
+        w_mx = (first_codes[:, :P], first_scales[:, :P])
+        for n, (e0, moving) in enumerate((
+            (0, (first_codes[:, P:], first_scales[:, P:])),
+            (P, (middle_codes[:], middle_scales[:])),
+            (3 * P, (last_codes[:], last_scales[:])),
+        )):
+            width = moving[1].shape[1]
+            bank = ps.tile([P, width], F32, name="out_bank", tag="shared%d" % n)
+            product(bank[:], w_mx, moving)
+            result = sb.tile([P, width], F32, name="result%d" % n, tag="tail" if n == 0 else "result%d" % n)
+            nc.scalar.copy(result[:], bank[:])
+            nc.sync.dma_start(out[:, e0 : e0 + width], result[:])

@@ -37,10 +37,11 @@ def tile_attend_antiquery_kernel(tc, query, avoid, keys_words, keys_scales, aver
         ident = sb.tile([P, P], F32, name="ident")
 
         nc.vector.memset(key_bytes[:].bitcast(I32), 0)
-        make_identity(nc, ident[:])
+        nc.vector.memset(ident[:], 0.0)
+        make_identity(nc, ident[:], nomemset=True)
         with tc.tile_pool(name="early", bufs=1) as early:
             aver_col = early.tile([P, 1], F32, name="aver_col")
-            nc.scalar.dma_start(aver_col[:], aver)
+            nc.sync.dma_start(aver_col[:], aver)
             nc.sync.dma_start(offsets[:], offs)
             nc.sync.dma_start(key_words[:].bitcast(I32), keys_words[0].rearrange("p t r -> p (t r)").bitcast(I32))
             for n, source in enumerate((avoid, query)):

from contextlib import ExitStack

import concourse.mybir as mybir
from concourse.masks import make_identity

D, T, I, Q, E = 512, 2048, 512, 128, 512
FLOPS = 2 * Q * I * (2 * D + E)

F32 = mybir.dt.float32
BF16 = mybir.dt.bfloat16
I32 = mybir.dt.int32
U32 = mybir.dt.uint32
U16 = mybir.dt.uint16
U8 = mybir.dt.uint8
FP8X4 = mybir.dt.float8_e4m3fn_x4
ALU = mybir.AluOpType
ACT = mybir.ActivationFunctionType

P = 128
PACK = 4
QUADRANT = 32
WINDOW_BYTES = 4 * T
ALIGN = 64


def tile_attend_antiquery_kernel(tc, query, avoid, keys_words, keys_scales, aver, size, vals, offs, out):
    nc = tc.nc
    with ExitStack() as ctx:
        sb = ctx.enter_context(tc.tile_pool(name="sb", bufs=1))
        ps = ctx.enter_context(tc.psum_pool(name="ps", bufs=1))

        offsets = sb.tile([P, I // 16], U16, name="offsets")
        key_words = sb.tile([P, T], U32, name="key_words", tag="keys", align_bytes=ALIGN)
        key_bytes = sb.tile([P, T], U8, name="key_bytes", align_bytes=ALIGN)
        rows = [sb.tile([P, PACK, Q], F32, name="rows%d" % n) for n in range(2)]
        neg_aver = sb.tile([P, 1], F32, name="neg_aver")
        ident = sb.tile([P, P], F32, name="ident")

        nc.vector.memset(key_bytes[:].bitcast(I32), 0)
        nc.vector.memset(ident[:], 0.0)
        make_identity(nc, ident[:], nomemset=True)
        with tc.tile_pool(name="early", bufs=1) as early:
            aver_col = early.tile([P, 1], F32, name="aver_col")
            nc.sync.dma_start(aver_col[:], aver)
            nc.sync.dma_start(offsets[:], offs)
            nc.sync.dma_start(key_words[:].bitcast(I32), keys_words[0].rearrange("p t r -> p (t r)").bitcast(I32))
            for n, source in enumerate((avoid, query)):
                nc.sync.dma_start(rows[n][:], source.rearrange("(p r) q -> p r q", r=PACK))
            for quad in range(P // QUADRANT):
                nc.scalar.dma_start(
                    key_bytes[QUADRANT * quad : QUADRANT * quad + 4, :].bitcast(I32),
                    keys_scales[0, 4 * quad : 4 * quad + 4, :].bitcast(I32),
                )
            nc.vector.tensor_scalar_mul(neg_aver[:], aver_col[:], -1.0)

        late = ctx.enter_context(tc.tile_pool(name="late", bufs=1))

        def late_tile(name, shape, dtype, window):
            return late.tile(shape, dtype, name=name, offset=window * WINDOW_BYTES, align_bytes=ALIGN)

        windows = [late_tile("window%d" % j, [P, T], F32, j) for j in range(E // P)]
        size_cols = late_tile("size_cols", [P, PACK], F32, E // P)
        for j in range(E // P):
            nc.sync.dma_start(windows[j][:], vals[j * P : (j + 1) * P, :])
            if j == 0:
                nc.sync.dma_start(size_cols[:], size.rearrange("o (p r) -> (o p) r", r=PACK))

        def quantise(name, grouped, codes):
            scales = sb.tile(list(codes.shape), U8, name=name + "_scales", align_bytes=ALIGN)
            nc.vector.quantize_mx(out=codes[:].bitcast(FP8X4), scales=scales[:], in_=grouped[:])
            return codes, scales

        def product(bank, stationary, moving):
            nc.tensor.matmul_mx(
                out=bank, lhsT=stationary[0].bitcast(FP8X4), lhsT_scale=stationary[1],
                rhs=moving[0].bitcast(FP8X4), rhs_scale=moving[1], start=True, stop=True,
            )

        k_words = sb.tile([P, I], U32, name="k_words", align_bytes=ALIGN)
        nc.vector.tensor_copy(k_words[:], key_words[:].indirect(offsets[:]))
        k_bytes = sb.tile([P, I], U8, name="k_bytes", tag="keys", align_bytes=ALIGN)
        nc.vector.tensor_copy(k_bytes[:], key_bytes[:].indirect(offsets[:]))

        rows_mx = []
        for n in range(2):
            grouped = sb.tile([P, Q * PACK], BF16, name="rows_grouped%d" % n, align_bytes=ALIGN)
            nc.scalar.activation(
                grouped[:].rearrange("p (q r) -> p q r", r=PACK), rows[n][:].rearrange("p r q -> p q r"), ACT.Copy
            )
            codes, scales = quantise("rows%d" % n, grouped, sb.tile([P, Q], U32, name="rows%d_codes" % n, align_bytes=ALIGN))
            rows_mx.append((codes[:], scales[:]))
        relu_b = sb.tile([P, I], F32, name="relu_b")
        for half in range(2):
            slots = slice(half * I // 2, (half + 1) * I // 2)
            b_bank = ps.tile([P, I // 2], F32, name="b_bank", tag="shared%d" % half)
            product(b_bank[:], rows_mx[0], (k_words[:, slots], k_bytes[:, slots]))
            nc.scalar.activation(relu_b[:, slots], b_bank[:], ACT.Relu)
        a_bank = ps.tile([P, I], F32, name="a_bank", tag="shared2")
        product(a_bank[:], rows_mx[1], (k_words[:], k_bytes[:]))

        size_bank = ps.tile([P, PACK, P], F32, name="size_bank")
        for r in range(PACK):
            nc.tensor.transpose(size_bank[:, r, :], size_cols[:, r : r + 1].to_broadcast([P, P]), ident[:])

        def turn(source, grouped):
            words = source[:].bitcast(F32)
            bank = ps.tile([P, 2, P], F32, name="turn", bufs=2)
            for u in range(2):
                nc.tensor.transpose(bank[:, u, :], words[:, u::2], ident[:])
            nc.scalar.copy(grouped.bitcast(F32).rearrange("p (x u) -> p x u", u=2), bank[:].rearrange("p u x -> p x u"))

        def gather(j, picked):
            nc.vector.tensor_copy(picked[:], windows[j][:].indirect(offsets[:]))
            return picked

        first = sb.tile([P, 2 * I], BF16, name="first", align_bytes=ALIGN)
        middle = sb.tile([P, 2 * I], BF16, name="middle", align_bytes=ALIGN)
        last = sb.tile([P, I], BF16, name="last", align_bytes=ALIGN)

        picked0 = gather(0, sb.tile([P, I], BF16, name="picked0"))
        s = late_tile("s", [P, I], F32, 0)
        nc.vector.scalar_tensor_tensor(s[:], relu_b[:], neg_aver[:], a_bank[:], ALU.mult, ALU.add)
        neg_max = sb.tile([P, 1], F32, name="neg_max")
        nc.vector.tensor_reduce(neg_max[:], s[:], mybir.AxisListType.X, ALU.max, negate=True)
        turn(picked0, first[:, I:])
        p = sb.tile([P, I], F32, name="p")
        total = sb.tile([P, 1], F32, name="total")
        nc.scalar.activation(p[:], s[:], ACT.Exp, bias=neg_max[:], accum_out=total[:])
        turn(gather(1, late_tile("picked1", [P, I], BF16, E // P)), middle[:, :I])
        inverse = late_tile("inverse", [P, 1], F32, 1)
        nc.vector.reciprocal(inverse[:], total[:])
        w = sb.tile([P, I], BF16, name="w", align_bytes=ALIGN)
        nc.vector.scalar_tensor_tensor(
            w[:].rearrange("q (p r) -> q p r", r=PACK), p[:].rearrange("q (p r) -> q p r", r=PACK), inverse[:],
            size_bank[:].rearrange("q r p -> q p r"), ALU.mult, ALU.mult,
        )
        turn(w, first[:, :I])
        turn(gather(2, sb.tile([P, I], BF16, name="picked2")), middle[:, I:])
        turn(gather(3, sb.tile([P, I], BF16, name="picked3", tag="tail")), last[:])

        first_codes, first_scales = quantise("first", first, late_tile("first_codes", [P, 2 * P], U32, 3))
        middle_codes, middle_scales = quantise("middle", middle, late.tile([P, 2 * P], U32, name="middle_codes", offset=3 * WINDOW_BYTES + 8 * P, align_bytes=ALIGN))
        last_codes, last_scales = quantise("last", last, sb.tile([P, P], U32, name="last_codes", align_bytes=ALIGN))
        w_mx = (first_codes[:, :P], first_scales[:, :P])
        for n, (e0, moving) in enumerate((
            (0, (first_codes[:, P:], first_scales[:, P:])),
            (P, (middle_codes[:], middle_scales[:])),
            (3 * P, (last_codes[:], last_scales[:])),
        )):
            width = moving[1].shape[1]
            bank = ps.tile([P, width], F32, name="out_bank", tag="shared%d" % n)
            product(bank[:], w_mx, moving)
            result = sb.tile([P, width], F32, name="result%d" % n, tag="tail" if n == 0 else "result%d" % n)
            nc.scalar.copy(result[:], bank[:])
            nc.sync.dma_start(out[:, e0 : e0 + width], result[:])
